import numpy as np
import ml_dtypes


def mxq(x, axis, fmt="e4m3"):
    dtype, down = {"e4m3": (ml_dtypes.float8_e4m3fn, 7), "e5m2": (ml_dtypes.float8_e5m2, 14)}[fmt]
    v = np.moveaxis(np.asarray(x, np.float32).astype(ml_dtypes.bfloat16).astype(np.float64), axis, -1)
    blocks = v.reshape(v.shape[:-1] + (-1, 32))
    amax = np.abs(blocks).max(-1, keepdims=True)
    byte = np.maximum(np.where(amax > 0, np.frexp(amax)[1] - 1 + 127, 0) - down, 1)
    scale = np.exp2(byte - 127.0)
    codes = (blocks / scale).astype(np.float32).astype(dtype).astype(np.float64)
    return np.moveaxis((codes * scale).reshape(v.shape), -1, axis)


WIDE = False


def mx_kscale(k):
    if not WIDE:
        return np.ones(k)
    levels = np.array([10, -10, 5, -5, 0])
    if k % 512:
        return np.exp2(np.random.permutation(np.resize(levels, k // 32))).repeat(32)
    a = np.empty((k // 512, 16))
    for p in range(k // 512):
        a[p, :8] = np.random.permutation(np.resize(levels, 8))
        for g in range(8):
            far = levels[np.abs(levels - a[p, g]) >= 10]
            a[p, g + 8] = far[np.random.randint(len(far))]
    return np.exp2(a.ravel()).repeat(32)


def f64(x):
    return np.asarray(x).astype(np.float64)


def striped(idx):
    return np.tile(idx.reshape(-1, 16).T, (8, 1)).astype(np.uint16)


def unstriped(offs):
    return offs[:16].T.reshape(-1).astype(np.int64)


def pack_weight(w):
    k, n = w.shape
    w = f64(np.asarray(w, np.float32).astype(ml_dtypes.bfloat16)).reshape(k // 32, 32, n)
    amax = np.abs(w).max(1)
    byte = np.clip(np.where(amax > 0, np.frexp(amax)[1] - 1 + 127 - 7, 1), 1, 254)
    scaled = (w * np.exp2(127.0 - byte)[:, None, :]).reshape(k, n).astype(np.float32)
    words = np.ascontiguousarray(scaled.reshape(k // 512, 128, 4, n).transpose(0, 1, 3, 2)).astype(ml_dtypes.float8_e4m3fn).view(np.uint8)
    return words, np.ascontiguousarray(byte.astype(np.uint8).reshape(k // 512, 16, n))


def unpack_weight(words, scales):
    g, p, n, _ = words.shape
    vals = np.ascontiguousarray(words).view(ml_dtypes.float8_e4m3fn).astype(np.float64) * np.repeat(np.exp2(scales.astype(np.float64) - 127.0), 8, axis=1)[..., None]
    return vals.transpose(0, 1, 3, 2).reshape(g * 512, n)


def relu(v):
    return np.maximum(v, 0.0)


K, T, S, N, D = 1024, 1024, 512, 128, 2
P = 2 ** 7


def setup_inputs():
    n = np.random.standard_normal
    s = mx_kscale(K)[:, None]
    packed_xT = pack_weight(n((K, T)) * s)
    return {
        "x_words": packed_xT[0],
        "x_scales": packed_xT[1],
        "w1": (n((K, N)) / np.sqrt(K) / s).astype(np.float32),
        "gate": (np.tile(np.random.uniform(0.3, 0.6, (D, 1, S)), (1, P, 1))).astype(np.float32),
        "pos0": (n((N, S))).astype(np.float32),
        "vel0": (n((N, S))).astype(np.float32),
        "offs": striped(np.random.permutation(T)[:S]),
        "pos1": striped(np.random.permutation(S)[:S]),
        "pos2": striped(np.random.permutation(S)[:S]),
    }


def reference(x_words, x_scales, w1, gate, pos0, vel0, offs, pos1, pos2):
    xq = unpack_weight(x_words, x_scales)[:, unstriped(offs)]
    y = mxq(f64(w1), 0, "e4m3").T @ xq
    gg = y[:, unstriped(pos1)] * f64(gate)[0, :1] + y[:, unstriped(pos2)] * f64(gate)[1, :1]
    vel = f64(vel0) + 0.7 * (relu(gg) - f64(pos0) - (0.5 * f64(vel0)))
    return f64(pos0) + 0.7 * vel

@@ -1,0 +1,140 @@
+from contextlib import ExitStack
+
+import concourse.mybir as mybir
+
+K, T, S, N = 1024, 1024, 512, 128
+FLOPS = 2 * K * N * S
+
+F32 = mybir.dt.float32
+BF16 = mybir.dt.bfloat16
+I32 = mybir.dt.int32
+U32 = mybir.dt.uint32
+U16 = mybir.dt.uint16
+U8 = mybir.dt.uint8
+FP8X4 = mybir.dt.float8_e4m3fn_x4
+ALU = mybir.AluOpType
+COPY = mybir.ActivationFunctionType.Copy
+
+P = 128
+PACK = 4
+PASSES = K // (P * PACK)
+LIST_COL = 16
+DT = 0.7
+C_FORCE = DT * DT
+C_POS = 1.0 - DT * DT
+C_VEL = DT - 0.5 * DT * DT
+Y_PIECES = ((0, 256), (256, 384), (384, 512))
+OUT_PIECES = ((0, 256), (256, 512))
+
+
+def entries(list_tile, lo, hi):
+    return list_tile[:, lo // LIST_COL : hi // LIST_COL]
+
+
+def tile_picked_ygcon_relu_p_kernel(
+    tc, x_words, x_scales, w1, gate, pos0, vel0, offs, pos1, pos2, out
+):
+    nc = tc.nc
+    with ExitStack() as ctx:
+        keep = ctx.enter_context(tc.tile_pool(name="keep", bufs=1))
+        psum = ctx.enter_context(tc.psum_pool(name="psum", bufs=1))
+
+        offs_sb = keep.tile([P, S // LIST_COL], U16, name="offs_sb")
+        pos_sb = [keep.tile([P, S // LIST_COL], U16, name="pos_sb%d" % d) for d in range(2)]
+        scale_table = keep.tile([P, T], U8, name="scale_table", align_bytes=64)
+        warm_in = keep.tile([P, 1], F32, name="warm_in")
+        warm_out = keep.tile([P, 1], F32, name="warm_out")
+
+        nc.vector.memset(scale_table[:].bitcast(I32), 0)
+        nc.vector.memset(warm_in[:], 0.0)
+        nc.sync.dma_start(offs_sb[:], offs)
+        for q in range(4):
+            nc.scalar.dma_start(
+                out=scale_table[32 * q : 32 * q + 4 * PASSES, :].bitcast(I32),
+                in_=x_scales[:, 4 * q : 4 * q + 4, :].bitcast(I32),
+            )
+        nc.scalar.activation(warm_out[:], warm_in[:], COPY)
+
+        w_raw = []
+        for g in range(PASSES):
+            raw = keep.tile([P, PACK, N], F32, name="w_raw%d" % g)
+            nc.sync.dma_start(out=raw[:], in_=w1[g * P * PACK : (g + 1) * P * PACK, :].rearrange("(p j) m -> p j m", j=PACK))
+            w_raw.append(raw)
+        word_table = []
+        for g in range(PASSES):
+            table = keep.tile([P, T], I32, name="word_table%d" % g, align_bytes=64)
+            nc.sync.dma_start(out=table[:], in_=x_words[g].rearrange("p c t -> p (c t)").bitcast(I32))
+            word_table.append(table)
+        pos0_sb = keep.tile([P, S], F32, name="pos0_sb")
+        vel0_sb = keep.tile([P, S], F32, name="vel0_sb")
+        nc.sync.dma_start(out=pos0_sb[:], in_=pos0)
+        nc.sync.dma_start(out=vel0_sb[:], in_=vel0)
+        nc.sync.dma_start(pos_sb[0][:], pos1)
+        nc.sync.dma_start(pos_sb[1][:], pos2)
+        gate_sb = []
+        for d in range(2):
+            weights = keep.tile([P, S], F32, name="gate_sb%d" % d)
+            nc.sync.dma_start(out=weights[:], in_=gate[d])
+            gate_sb.append(weights)
+
+        x_scale = keep.tile([P, S], U8, name="x_scale", align_bytes=64)
+        nc.vector.tensor_copy(x_scale[:], scale_table[:].indirect(offs_sb[:]))
+
+        w_codes, w_scale = [], []
+        for g in range(PASSES):
+            grouped = keep.tile([P, N, PACK], BF16, name="w_grouped%d" % g, align_bytes=64)
+            nc.scalar.activation(grouped[:], w_raw[g][:].rearrange("p j m -> p m j"), COPY)
+            codes = keep.tile([P, N], U32, name="w_codes%d" % g, align_bytes=64)
+            plane = keep.tile([P, N], U8, name="w_scale%d" % g, align_bytes=64)
+            nc.vector.quantize_mx(out=codes[:].bitcast(FP8X4), scales=plane[:], in_=grouped[:].rearrange("p m j -> p (m j)"))
+            w_codes.append(codes)
+            w_scale.append(plane)
+
+        y_sb = keep.tile([P, S], F32, name="y_sb")
+        acc = [psum.tile([P, hi - lo], F32, name="acc%d" % lo) for lo, hi in Y_PIECES]
+        x_codes = [keep.tile([P, S], U32, name="x_codes%d" % g, align_bytes=64) for g in range(PASSES)]
+        for g in range(PASSES):
+            last = g == PASSES - 1
+            for lo, hi in (Y_PIECES if last else ((0, S),)):
+                nc.vector.tensor_copy(x_codes[g][:, lo:hi], word_table[g][:].bitcast(U32).indirect(entries(offs_sb, lo, hi)))
+            for i, (lo, hi) in enumerate(Y_PIECES):
+                nc.tensor.matmul_mx(
+                    out=acc[i][:],
+                    lhsT=w_codes[g][:].bitcast(FP8X4),
+                    lhsT_scale=w_scale[g][:],
+                    rhs=x_codes[g][:, lo:hi].bitcast(FP8X4),
+                    rhs_scale=x_scale[4 * g : P, lo:hi],
+                    start=(g == 0),
+                    stop=last,
+                )
+        for i, (lo, hi) in enumerate(Y_PIECES):
+            nc.scalar.activation(y_sb[:, lo:hi], acc[i][:], COPY, scale=C_FORCE)
+
+        mixed = keep.tile([P, S], F32, name="mixed")
+        base = keep.tile([P, S], F32, name="base")
+        nc.vector.scalar_tensor_tensor(mixed[:], pos0_sb[:], C_POS / C_VEL, vel0_sb[:], ALU.mult, ALU.add)
+        nc.scalar.activation(base[:], mixed[:], COPY, scale=C_VEL)
+
+        pulled = [keep.tile([P, S], F32, name="pulled%d" % d) for d in range(2)]
+        total = keep.tile([P, S], F32, name="total")
+        result = keep.tile([P, S], F32, name="result")
+
+        def fetch(d, lo, hi):
+            nc.vector.tensor_tensor(pulled[d][:, lo:hi], y_sb[:].indirect(entries(pos_sb[d], lo, hi)), gate_sb[d][:, lo:hi], ALU.mult)
+
+        def add(lo, hi):
+            nc.vector.tensor_tensor(total[:, lo:hi], pulled[0][:, lo:hi], pulled[1][:, lo:hi], ALU.add)
+
+        def finish(lo, hi):
+            nc.vector.scalar_tensor_tensor(result[:, lo:hi], total[:, lo:hi], 0.0, base[:, lo:hi], ALU.max, ALU.add)
+            nc.sync.dma_start(out=out[:, lo:hi], in_=result[:, lo:hi])
+
+        first, second = OUT_PIECES
+        fetch(0, *first)
+        fetch(1, *first)
+        fetch(0, *second)
+        add(*first)
+        fetch(1, *second)
+        finish(*first)
+        add(*second)
+        finish(*second)

@@ -24,7 +24,8 @@ C_FORCE = DT * DT
 C_POS = 1.0 - DT * DT
 C_VEL = DT - 0.5 * DT * DT
 Y_PIECES = ((0, 256), (256, 384), (384, 512))
-OUT_PIECES = ((0, 256), (256, 512))
+GATHER_PIECES = ((0, 384), (384, 512))
+SPARE = 16
 
 
 def entries(list_tile, lo, hi):
@@ -48,35 +49,37 @@ def tile_picked_ygcon_relu_p_kernel(
         nc.vector.memset(scale_table[:].bitcast(I32), 0)
         nc.vector.memset(warm_in[:], 0.0)
         nc.sync.dma_start(offs_sb[:], offs)
+        nc.scalar.activation(warm_out[:], warm_in[:], COPY)
+
+        word_table = [keep.tile([P, T], I32, name="word_table%d" % g, align_bytes=64) for g in range(PASSES)]
+        w_raw = [keep.tile([P, PACK, N], F32, name="w_raw%d" % g) for g in range(PASSES)]
+
+        def load_words(g):
+            nc.sync.dma_start(out=word_table[g][:], in_=x_words[g].rearrange("p c t -> p (c t)").bitcast(I32))
+
+        load_words(0)
         for q in range(4):
-            nc.scalar.dma_start(
+            nc.sync.dma_start(
                 out=scale_table[32 * q : 32 * q + 4 * PASSES, :].bitcast(I32),
                 in_=x_scales[:, 4 * q : 4 * q + 4, :].bitcast(I32),
             )
-        nc.scalar.activation(warm_out[:], warm_in[:], COPY)
-
-        w_raw = []
         for g in range(PASSES):
-            raw = keep.tile([P, PACK, N], F32, name="w_raw%d" % g)
-            nc.sync.dma_start(out=raw[:], in_=w1[g * P * PACK : (g + 1) * P * PACK, :].rearrange("(p j) m -> p j m", j=PACK))
-            w_raw.append(raw)
-        word_table = []
-        for g in range(PASSES):
-            table = keep.tile([P, T], I32, name="word_table%d" % g, align_bytes=64)
-            nc.sync.dma_start(out=table[:], in_=x_words[g].rearrange("p c t -> p (c t)").bitcast(I32))
-            word_table.append(table)
+            nc.sync.dma_start(out=w_raw[g][:], in_=w1[g * P * PACK : (g + 1) * P * PACK, :].rearrange("(p j) m -> p j m", j=PACK))
+        load_words(1)
         pos0_sb = keep.tile([P, S], F32, name="pos0_sb")
         vel0_sb = keep.tile([P, S], F32, name="vel0_sb")
-        nc.sync.dma_start(out=pos0_sb[:], in_=pos0)
-        nc.sync.dma_start(out=vel0_sb[:], in_=vel0)
         nc.sync.dma_start(pos_sb[0][:], pos1)
         nc.sync.dma_start(pos_sb[1][:], pos2)
+        nc.sync.dma_start(out=pos0_sb[:], in_=pos0)
+        nc.sync.dma_start(out=vel0_sb[:], in_=vel0)
         gate_sb = []
         for d in range(2):
             weights = keep.tile([P, S], F32, name="gate_sb%d" % d)
             nc.sync.dma_start(out=weights[:], in_=gate[d])
             gate_sb.append(weights)
 
+        x_codes = [keep.tile([P, S], U32, name="x_codes%d" % g, align_bytes=64) for g in range(PASSES)]
+        nc.vector.tensor_copy(x_codes[0][:], word_table[0][:].bitcast(U32).indirect(offs_sb[:]))
         x_scale = keep.tile([P, S], U8, name="x_scale", align_bytes=64)
         nc.vector.tensor_copy(x_scale[:], scale_table[:].indirect(offs_sb[:]))
 
@@ -90,12 +93,12 @@ def tile_picked_ygcon_relu_p_kernel(
             w_codes.append(codes)
             w_scale.append(plane)
 
-        y_sb = keep.tile([P, S], F32, name="y_sb")
+        y_sb = keep.tile([P, S + SPARE], F32, name="y_sb")
+        nc.gpsimd.memset(y_sb[:, S:], 0.0)
         acc = [psum.tile([P, hi - lo], F32, name="acc%d" % lo) for lo, hi in Y_PIECES]
-        x_codes = [keep.tile([P, S], U32, name="x_codes%d" % g, align_bytes=64) for g in range(PASSES)]
         for g in range(PASSES):
             last = g == PASSES - 1
-            for lo, hi in (Y_PIECES if last else ((0, S),)):
+            for lo, hi in (GATHER_PIECES if last else ()):
                 nc.vector.tensor_copy(x_codes[g][:, lo:hi], word_table[g][:].bitcast(U32).indirect(entries(offs_sb, lo, hi)))
             for i, (lo, hi) in enumerate(Y_PIECES):
                 nc.tensor.matmul_mx(
@@ -129,12 +132,13 @@ def tile_picked_ygcon_relu_p_kernel(
             nc.vector.scalar_tensor_tensor(result[:, lo:hi], total[:, lo:hi], 0.0, base[:, lo:hi], ALU.max, ALU.add)
             nc.sync.dma_start(out=out[:, lo:hi], in_=result[:, lo:hi])
 
-        first, second = OUT_PIECES
-        fetch(0, *first)
-        fetch(1, *first)
-        fetch(0, *second)
-        add(*first)
-        fetch(1, *second)
-        finish(*first)
-        add(*second)
-        finish(*second)
+        half, quarter = S // 2, S // 4
+        fetch(0, 0, S)
+        fetch(1, 0, half)
+        fetch(1, half, S)
+        add(0, half)
+        add(half, S - quarter)
+        finish(0, half)
+        add(S - quarter, S)
+        finish(half, S - quarter)
+        finish(S - quarter, S)

@@ -24,7 +24,6 @@ C_FORCE = DT * DT
 C_POS = 1.0 - DT * DT
 C_VEL = DT - 0.5 * DT * DT
 Y_PIECES = ((0, 256), (256, 384), (384, 512))
-GATHER_PIECES = ((0, 384), (384, 512))
 SPARE = 16
 
 
@@ -52,7 +51,7 @@ def tile_picked_ygcon_relu_p_kernel(
         nc.scalar.activation(warm_out[:], warm_in[:], COPY)
 
         word_table = [keep.tile([P, T], I32, name="word_table%d" % g, align_bytes=64) for g in range(PASSES)]
-        w_raw = [keep.tile([P, PACK, N], F32, name="w_raw%d" % g) for g in range(PASSES)]
+        w_raw = [keep.tile([P, PACK, N], F32, name="w_raw%d" % g, tag="w_slot%d" % g, align_bytes=64) for g in range(PASSES)]
 
         def load_words(g):
             nc.sync.dma_start(out=word_table[g][:], in_=x_words[g].rearrange("p c t -> p (c t)").bitcast(I32))
@@ -68,18 +67,18 @@ def tile_picked_ygcon_relu_p_kernel(
         load_words(1)
         pos0_sb = keep.tile([P, S], F32, name="pos0_sb")
         vel0_sb = keep.tile([P, S], F32, name="vel0_sb")
+        nc.sync.dma_start(out=vel0_sb[:], in_=vel0)
+        nc.sync.dma_start(out=pos0_sb[:], in_=pos0)
         nc.sync.dma_start(pos_sb[0][:], pos1)
         nc.sync.dma_start(pos_sb[1][:], pos2)
-        nc.sync.dma_start(out=pos0_sb[:], in_=pos0)
-        nc.sync.dma_start(out=vel0_sb[:], in_=vel0)
         gate_sb = []
         for d in range(2):
             weights = keep.tile([P, S], F32, name="gate_sb%d" % d)
             nc.sync.dma_start(out=weights[:], in_=gate[d])
             gate_sb.append(weights)
 
-        x_codes = [keep.tile([P, S], U32, name="x_codes%d" % g, align_bytes=64) for g in range(PASSES)]
-        nc.vector.tensor_copy(x_codes[0][:], word_table[0][:].bitcast(U32).indirect(offs_sb[:]))
+        x_first = keep.tile([P, S], U32, name="x_first", align_bytes=64)
+        nc.vector.tensor_copy(x_first[:], word_table[0][:].bitcast(U32).indirect(offs_sb[:]))
         x_scale = keep.tile([P, S], U8, name="x_scale", align_bytes=64)
         nc.vector.tensor_copy(x_scale[:], scale_table[:].indirect(offs_sb[:]))
 
@@ -93,19 +92,28 @@ def tile_picked_ygcon_relu_p_kernel(
             w_codes.append(codes)
             w_scale.append(plane)
 
+        damped = keep.tile([P, S], F32, name="damped")
+        nc.scalar.activation(damped[:], vel0_sb[:], COPY, scale=C_VEL)
+
         y_sb = keep.tile([P, S + SPARE], F32, name="y_sb")
         nc.gpsimd.memset(y_sb[:, S:], 0.0)
         acc = [psum.tile([P, hi - lo], F32, name="acc%d" % lo) for lo, hi in Y_PIECES]
+        x_early = keep.tile([P, S // 2], U32, name="x_early", align_bytes=64)
+        x_late = keep.tile([P, S // 2], U32, name="x_late", tag="w_slot1", align_bytes=64)
+        x_codes = [
+            [x_first[:, lo:hi] for lo, hi in Y_PIECES],
+            [x_early[:], x_late[:, 0:128], x_late[:, 128:256]],
+        ]
         for g in range(PASSES):
             last = g == PASSES - 1
-            for lo, hi in (GATHER_PIECES if last else ()):
-                nc.vector.tensor_copy(x_codes[g][:, lo:hi], word_table[g][:].bitcast(U32).indirect(entries(offs_sb, lo, hi)))
+            for i, (lo, hi) in enumerate(Y_PIECES if last else ()):
+                nc.vector.tensor_copy(x_codes[g][i], word_table[g][:].bitcast(U32).indirect(entries(offs_sb, lo, hi)))
             for i, (lo, hi) in enumerate(Y_PIECES):
                 nc.tensor.matmul_mx(
                     out=acc[i][:],
                     lhsT=w_codes[g][:].bitcast(FP8X4),
                     lhsT_scale=w_scale[g][:],
-                    rhs=x_codes[g][:, lo:hi].bitcast(FP8X4),
+                    rhs=x_codes[g][i].bitcast(FP8X4),
                     rhs_scale=x_scale[4 * g : P, lo:hi],
                     start=(g == 0),
                     stop=last,
@@ -113,10 +121,8 @@ def tile_picked_ygcon_relu_p_kernel(
         for i, (lo, hi) in enumerate(Y_PIECES):
             nc.scalar.activation(y_sb[:, lo:hi], acc[i][:], COPY, scale=C_FORCE)
 
-        mixed = keep.tile([P, S], F32, name="mixed")
         base = keep.tile([P, S], F32, name="base")
-        nc.vector.scalar_tensor_tensor(mixed[:], pos0_sb[:], C_POS / C_VEL, vel0_sb[:], ALU.mult, ALU.add)
-        nc.scalar.activation(base[:], mixed[:], COPY, scale=C_VEL)
+        nc.vector.scalar_tensor_tensor(base[:], pos0_sb[:], C_POS, damped[:], ALU.mult, ALU.add)
 
         pulled = [keep.tile([P, S], F32, name="pulled%d" % d) for d in range(2)]
         total = keep.tile([P, S], F32, name="total")
@@ -128,17 +134,16 @@ def tile_picked_ygcon_relu_p_kernel(
         def add(lo, hi):
             nc.vector.tensor_tensor(total[:, lo:hi], pulled[0][:, lo:hi], pulled[1][:, lo:hi], ALU.add)
 
-        def finish(lo, hi):
+        def finish(lo, hi, queue):
             nc.vector.scalar_tensor_tensor(result[:, lo:hi], total[:, lo:hi], 0.0, base[:, lo:hi], ALU.max, ALU.add)
-            nc.sync.dma_start(out=out[:, lo:hi], in_=result[:, lo:hi])
+            queue.dma_start(out=out[:, lo:hi], in_=result[:, lo:hi])
 
         half, quarter = S // 2, S // 4
         fetch(0, 0, S)
         fetch(1, 0, half)
         fetch(1, half, S)
         add(0, half)
-        add(half, S - quarter)
-        finish(0, half)
-        add(S - quarter, S)
-        finish(half, S - quarter)
-        finish(S - quarter, S)
+        add(half, S)
+        finish(0, half, nc.sync)
+        finish(half, S - quarter, nc.scalar)
+        finish(S - quarter, S, nc.sync)

@@ -145,5 +145,5 @@ def tile_picked_ygcon_relu_p_kernel(
         add(0, half)
         add(half, S)
         finish(0, half, nc.sync)
-        finish(half, S - quarter, nc.scalar)
+        finish(half, S - quarter, nc.sync)
         finish(S - quarter, S, nc.sync)

@@ -1,6 +1,7 @@
 from contextlib import ExitStack
 
 import concourse.mybir as mybir
+from concourse.masks import make_identity
 
 K, T, S, N = 1024, 1024, 512, 128
 FLOPS = 2 * K * N * S
@@ -14,6 +15,7 @@ U8 = mybir.dt.uint8
 FP8X4 = mybir.dt.float8_e4m3fn_x4
 ALU = mybir.AluOpType
 COPY = mybir.ActivationFunctionType.Copy
+RELU = mybir.ActivationFunctionType.Relu
 
 P = 128
 PACK = 4
@@ -72,9 +74,9 @@ def tile_picked_ygcon_relu_p_kernel(
         nc.sync.dma_start(pos_sb[0][:], pos1)
         nc.sync.dma_start(pos_sb[1][:], pos2)
         gate_sb = []
-        for d in range(2):
-            weights = keep.tile([P, S], F32, name="gate_sb%d" % d)
-            nc.sync.dma_start(out=weights[:], in_=gate[d])
+        for h in range(2):
+            weights = keep.tile([P, 2, S // 2], F32, name="gate_sb%d" % h)
+            nc.sync.dma_start(out=weights[:], in_=gate[:, :, h * (S // 2) : (h + 1) * (S // 2)].rearrange("d p j -> p d j"))
             gate_sb.append(weights)
 
         x_first = keep.tile([P, S], U32, name="x_first", align_bytes=64)
@@ -129,7 +131,7 @@ def tile_picked_ygcon_relu_p_kernel(
         result = keep.tile([P, S], F32, name="result")
 
         def fetch(d, lo, hi):
-            nc.vector.tensor_tensor(pulled[d][:, lo:hi], y_sb[:].indirect(entries(pos_sb[d], lo, hi)), gate_sb[d][:, lo:hi], ALU.mult)
+            nc.vector.tensor_tensor(pulled[d][:, lo:hi], y_sb[:].indirect(entries(pos_sb[d], lo, hi)), gate_sb[lo // (S // 2)][:, d, lo % (S // 2) : lo % (S // 2) + hi - lo], ALU.mult)
 
         def add(lo, hi):
             nc.vector.tensor_tensor(total[:, lo:hi], pulled[0][:, lo:hi], pulled[1][:, lo:hi], ALU.add)
@@ -139,11 +141,42 @@ def tile_picked_ygcon_relu_p_kernel(
             queue.dma_start(out=out[:, lo:hi], in_=result[:, lo:hi])
 
         half, quarter = S // 2, S // 4
-        fetch(0, 0, S)
-        fetch(1, 0, half)
-        fetch(1, half, S)
-        add(0, half)
-        add(half, S)
-        finish(0, half, nc.sync)
-        finish(half, S - quarter, nc.sync)
-        finish(S - quarter, S, nc.sync)
+        ident = keep.tile([P, P], F32, name="ident")
+        make_identity(nc, ident[:])
+
+        def turn(dst, src, start, stop):
+            nc.tensor.matmul(dst, src, ident[:], start=start, stop=stop, is_transpose=True)
+
+        base_turned_ps = psum.tile([P, half], F32, name="base_turned_ps")
+        for lo in (0, quarter):
+            turn(base_turned_ps[:, lo : lo + P], base[:, lo : lo + P], True, True)
+        base_turned = keep.tile([P, half], F32, name="base_turned")
+        nc.scalar.activation(base_turned[:], base_turned_ps[:], COPY)
+
+        blocks = (0, quarter)
+        sum_ps = [psum.tile([P, P], F32, name="sum_ps%d" % lo) for lo in blocks]
+        out_ps = [psum.tile([P, P], F32, name="out_ps%d" % lo) for lo in blocks]
+        force = [keep.tile([P, P], F32, name="force%d" % lo) for lo in blocks]
+        done = [keep.tile([P, P], F32, name="done%d" % lo) for lo in blocks]
+        fetch(0, 0, half)
+        for i, lo in enumerate(blocks):
+            turn(out_ps[i][:], base_turned[:, lo : lo + P], True, False)
+        for i, lo in enumerate(blocks):
+            turn(sum_ps[i][:], pulled[0][:, lo : lo + P], True, False)
+        for i, lo in enumerate(blocks):
+            fetch(1, lo, lo + P)
+            turn(sum_ps[i][:], pulled[1][:, lo : lo + P], False, True)
+            nc.scalar.activation(force[i][:], sum_ps[i][:], RELU)
+        for i, lo in enumerate(blocks):
+            turn(out_ps[i][:], force[i][:], False, True)
+            nc.scalar.activation(done[i][:], out_ps[i][:], COPY)
+            nc.sync.dma_start(out=out[:, lo : lo + P], in_=done[i][:])
+
+        fetch(0, half, S)
+        cut = S - 64
+        fetch(1, half, cut)
+        fetch(1, cut, S)
+        add(half, cut)
+        add(cut, S)
+        finish(half, cut, nc.sync)
+        finish(cut, S, nc.sync)

@@ -26,7 +26,6 @@ C_FORCE = DT * DT
 C_POS = 1.0 - DT * DT
 C_VEL = DT - 0.5 * DT * DT
 Y_PIECES = ((0, 256), (256, 384), (384, 512))
-SPARE = 16
 
 
 def entries(list_tile, lo, hi):
@@ -49,6 +48,9 @@ def tile_picked_ygcon_relu_p_kernel(
 
         nc.vector.memset(scale_table[:].bitcast(I32), 0)
         nc.vector.memset(warm_in[:], 0.0)
+        ident = keep.tile([P, P], F32, name="ident")
+        nc.vector.memset(ident[:], 0.0)
+        make_identity(nc, ident[:], nomemset=True)
         nc.sync.dma_start(offs_sb[:], offs)
         nc.scalar.activation(warm_out[:], warm_in[:], COPY)
 
@@ -74,9 +76,9 @@ def tile_picked_ygcon_relu_p_kernel(
         nc.sync.dma_start(pos_sb[0][:], pos1)
         nc.sync.dma_start(pos_sb[1][:], pos2)
         gate_sb = []
-        for h in range(2):
-            weights = keep.tile([P, 2, S // 2], F32, name="gate_sb%d" % h)
-            nc.sync.dma_start(out=weights[:], in_=gate[:, :, h * (S // 2) : (h + 1) * (S // 2)].rearrange("d p j -> p d j"))
+        for lo, hi in ((0, P), (P, S)):
+            weights = keep.tile([P, 2, hi - lo], F32, name="gate_sb%d" % lo)
+            nc.sync.dma_start(out=weights[:], in_=gate[:, :, lo:hi].rearrange("d p j -> p d j"))
             gate_sb.append(weights)
 
         x_first = keep.tile([P, S], U32, name="x_first", align_bytes=64)
@@ -97,14 +99,12 @@ def tile_picked_ygcon_relu_p_kernel(
         damped = keep.tile([P, S], F32, name="damped")
         nc.scalar.activation(damped[:], vel0_sb[:], COPY, scale=C_VEL)
 
-        y_sb = keep.tile([P, S + SPARE], F32, name="y_sb")
-        nc.gpsimd.memset(y_sb[:, S:], 0.0)
+        y_sb = keep.tile([P, S], F32, name="y_sb")
         acc = [psum.tile([P, hi - lo], F32, name="acc%d" % lo) for lo, hi in Y_PIECES]
-        x_early = keep.tile([P, S // 2], U32, name="x_early", align_bytes=64)
-        x_late = keep.tile([P, S // 2], U32, name="x_late", tag="w_slot1", align_bytes=64)
+        x_late = keep.tile([P, S], U32, name="x_late", tag="w_slot1", align_bytes=64)
         x_codes = [
             [x_first[:, lo:hi] for lo, hi in Y_PIECES],
-            [x_early[:], x_late[:, 0:128], x_late[:, 128:256]],
+            [x_late[:, lo:hi] for lo, hi in Y_PIECES],
         ]
         for g in range(PASSES):
             last = g == PASSES - 1
@@ -131,7 +131,7 @@ def tile_picked_ygcon_relu_p_kernel(
         result = keep.tile([P, S], F32, name="result")
 
         def fetch(d, lo, hi):
-            nc.vector.tensor_tensor(pulled[d][:, lo:hi], y_sb[:].indirect(entries(pos_sb[d], lo, hi)), gate_sb[lo // (S // 2)][:, d, lo % (S // 2) : lo % (S // 2) + hi - lo], ALU.mult)
+            nc.vector.tensor_tensor(pulled[d][:, lo:hi], y_sb[:].indirect(entries(pos_sb[d], lo, hi)), (gate_sb[0][:, d, lo:hi] if lo < P else gate_sb[1][:, d, lo - P : hi - P]), ALU.mult)
 
         def add(lo, hi):
             nc.vector.tensor_tensor(total[:, lo:hi], pulled[0][:, lo:hi], pulled[1][:, lo:hi], ALU.add)
@@ -140,43 +140,37 @@ def tile_picked_ygcon_relu_p_kernel(
             nc.vector.scalar_tensor_tensor(result[:, lo:hi], total[:, lo:hi], 0.0, base[:, lo:hi], ALU.max, ALU.add)
             queue.dma_start(out=out[:, lo:hi], in_=result[:, lo:hi])
 
-        half, quarter = S // 2, S // 4
-        ident = keep.tile([P, P], F32, name="ident")
-        make_identity(nc, ident[:])
 
         def turn(dst, src, start, stop):
             nc.tensor.matmul(dst, src, ident[:], start=start, stop=stop, is_transpose=True)
 
-        base_turned_ps = psum.tile([P, half], F32, name="base_turned_ps")
-        for lo in (0, quarter):
-            turn(base_turned_ps[:, lo : lo + P], base[:, lo : lo + P], True, True)
-        base_turned = keep.tile([P, half], F32, name="base_turned")
+        base_turned_ps = psum.tile([P, P], F32, name="base_turned_ps")
+        turn(base_turned_ps[:], base[:, 0:P], True, True)
+        base_turned = keep.tile([P, P], F32, name="base_turned")
         nc.scalar.activation(base_turned[:], base_turned_ps[:], COPY)
 
-        blocks = (0, quarter)
-        sum_ps = [psum.tile([P, P], F32, name="sum_ps%d" % lo) for lo in blocks]
-        out_ps = [psum.tile([P, P], F32, name="out_ps%d" % lo) for lo in blocks]
-        force = [keep.tile([P, P], F32, name="force%d" % lo) for lo in blocks]
-        done = [keep.tile([P, P], F32, name="done%d" % lo) for lo in blocks]
-        fetch(0, 0, half)
-        for i, lo in enumerate(blocks):
-            turn(out_ps[i][:], base_turned[:, lo : lo + P], True, False)
-        for i, lo in enumerate(blocks):
-            turn(sum_ps[i][:], pulled[0][:, lo : lo + P], True, False)
-        for i, lo in enumerate(blocks):
-            fetch(1, lo, lo + P)
-            turn(sum_ps[i][:], pulled[1][:, lo : lo + P], False, True)
-            nc.scalar.activation(force[i][:], sum_ps[i][:], RELU)
-        for i, lo in enumerate(blocks):
-            turn(out_ps[i][:], force[i][:], False, True)
-            nc.scalar.activation(done[i][:], out_ps[i][:], COPY)
-            nc.sync.dma_start(out=out[:, lo : lo + P], in_=done[i][:])
+        sum_ps = psum.tile([P, P], F32, name="sum_ps")
+        out_ps = psum.tile([P, P], F32, name="out_ps")
+        force = keep.tile([P, P], F32, name="force")
+        done = keep.tile([P, P], F32, name="done")
+        fetch(0, 0, P)
+        fetch(1, 0, P)
+        turn(out_ps[:], base_turned[:], True, False)
+        turn(sum_ps[:], pulled[0][:, 0:P], True, False)
+        turn(sum_ps[:], pulled[1][:, 0:P], False, True)
+        nc.scalar.activation(force[:], sum_ps[:], RELU)
+        turn(out_ps[:], force[:], False, True)
+        nc.scalar.activation(done[:], out_ps[:], COPY)
+        nc.sync.dma_start(out=out[:, 0:P], in_=done[:])
 
-        fetch(0, half, S)
-        cut = S - 64
-        fetch(1, half, cut)
+        mid, cut = 2 * P, S - 64
+        fetch(0, P, S)
+        fetch(1, P, mid)
+        fetch(1, mid, cut)
+        add(P, mid)
         fetch(1, cut, S)
-        add(half, cut)
+        add(mid, cut)
+        finish(P, mid, nc.sync)
         add(cut, S)
-        finish(half, cut, nc.sync)
+        finish(mid, cut, nc.sync)
         finish(cut, S, nc.sync)

@@ -1,7 +1,6 @@
 from contextlib import ExitStack
 
 import concourse.mybir as mybir
-from concourse.masks import make_identity
 
 K, T, S, N = 1024, 1024, 512, 128
 FLOPS = 2 * K * N * S
@@ -19,6 +18,7 @@ RELU = mybir.ActivationFunctionType.Relu
 
 P = 128
 PACK = 4
+QUAD = 32
 PASSES = K // (P * PACK)
 LIST_COL = 16
 DT = 0.7
@@ -50,8 +50,18 @@ def tile_picked_ygcon_relu_p_kernel(
         nc.vector.memset(warm_in[:], 0.0)
         ident = keep.tile([P, P], F32, name="ident")
         nc.vector.memset(ident[:], 0.0)
-        make_identity(nc, ident[:], nomemset=True)
+        ones = keep.tile([P, QUAD], F32, name="ones")
+        col_no = keep.tile([P, QUAD], F32, name="col_no", align_bytes=64)
+        row_no = keep.tile([P, QUAD], F32, name="row_no", align_bytes=64)
+        nc.vector.memset(ones[:], 1.0)
+        nc.vector.tensor_tensor_scan(col_no[:], ones[:], ones[:], 0.0, ALU.mult, ALU.add)
+        nc.vector.transpose(row_no[:], col_no[:])
+        for q in range(P // QUAD):
+            rows = slice(q * QUAD, (q + 1) * QUAD)
+            nc.vector.tensor_tensor(ident[rows, rows], col_no[rows, :], row_no[rows, :], ALU.is_equal)
         nc.sync.dma_start(offs_sb[:], offs)
+        gate_cols = keep.tile([P, 2 * PACK], F32, name="gate_cols")
+        nc.sync.dma_start(out=gate_cols[:], in_=gate.rearrange("d p j -> (d p) j")[P - 1 : P + 1, :].rearrange("r (n t) -> (r n) t", t=2 * PACK))
         nc.scalar.activation(warm_out[:], warm_in[:], COPY)
 
         word_table = [keep.tile([P, T], I32, name="word_table%d" % g, align_bytes=64) for g in range(PASSES)]
@@ -69,17 +79,24 @@ def tile_picked_ygcon_relu_p_kernel(
         for g in range(PASSES):
             nc.sync.dma_start(out=w_raw[g][:], in_=w1[g * P * PACK : (g + 1) * P * PACK, :].rearrange("(p j) m -> p j m", j=PACK))
         load_words(1)
-        pos0_sb = keep.tile([P, S], F32, name="pos0_sb")
-        vel0_sb = keep.tile([P, S], F32, name="vel0_sb")
+        pos0_sb = keep.tile([P, S], F32, name="pos0_sb", tag="sum_slot1")
+        vel0_sb = keep.tile([P, S], F32, name="vel0_sb", tag="y_slot")
         nc.sync.dma_start(out=vel0_sb[:], in_=vel0)
-        nc.sync.dma_start(out=pos0_sb[:], in_=pos0)
         nc.sync.dma_start(pos_sb[0][:], pos1)
         nc.sync.dma_start(pos_sb[1][:], pos2)
-        gate_sb = []
-        for lo, hi in ((0, P), (P, S)):
-            weights = keep.tile([P, 2, hi - lo], F32, name="gate_sb%d" % lo)
-            nc.sync.dma_start(out=weights[:], in_=gate[:, :, lo:hi].rearrange("d p j -> p d j"))
-            gate_sb.append(weights)
+        nc.sync.dma_start(out=pos0_sb[:], in_=pos0)
+
+        def turn(dst, src, start, stop):
+            nc.tensor.matmul(dst, src, ident[:], start=start, stop=stop, is_transpose=True)
+
+        gates = keep.tile([P, 2 * S], F32, name="gates")
+        for h in range(2):
+            spread = psum.tile([P, PACK, P], F32, name="spread%d" % h)
+            for t in range(PACK):
+                turn(spread[:, t, :], gate_cols[:, PACK * h + t : PACK * h + t + 1].to_broadcast([P, P]), True, True)
+            nc.scalar.activation(
+                gates[:].rearrange("p (n t) -> p n t", t=2 * PACK)[:, :, PACK * h : PACK * (h + 1)], spread[:].rearrange("p t n -> p n t"), COPY
+            )
 
         x_first = keep.tile([P, S], U32, name="x_first", align_bytes=64)
         nc.vector.tensor_copy(x_first[:], word_table[0][:].bitcast(U32).indirect(offs_sb[:]))
@@ -96,10 +113,10 @@ def tile_picked_ygcon_relu_p_kernel(
             w_codes.append(codes)
             w_scale.append(plane)
 
-        damped = keep.tile([P, S], F32, name="damped")
+        damped = keep.tile([P, S], F32, name="damped", tag="sum_slot0")
         nc.scalar.activation(damped[:], vel0_sb[:], COPY, scale=C_VEL)
 
-        y_sb = keep.tile([P, S], F32, name="y_sb")
+        y_sb = keep.tile([P, S], F32, name="y_sb", tag="y_slot")
         acc = [psum.tile([P, hi - lo], F32, name="acc%d" % lo) for lo, hi in Y_PIECES]
         x_late = keep.tile([P, S], U32, name="x_late", tag="w_slot1", align_bytes=64)
         x_codes = [
@@ -126,12 +143,12 @@ def tile_picked_ygcon_relu_p_kernel(
         base = keep.tile([P, S], F32, name="base")
         nc.vector.scalar_tensor_tensor(base[:], pos0_sb[:], C_POS, damped[:], ALU.mult, ALU.add)
 
-        pulled = [keep.tile([P, S], F32, name="pulled%d" % d) for d in range(2)]
+        pulled = [keep.tile([P, S], F32, name="pulled%d" % d, tag="sum_slot%d" % d) for d in range(2)]
         total = keep.tile([P, S], F32, name="total")
         result = keep.tile([P, S], F32, name="result")
 
         def fetch(d, lo, hi):
-            nc.vector.tensor_tensor(pulled[d][:, lo:hi], y_sb[:].indirect(entries(pos_sb[d], lo, hi)), (gate_sb[0][:, d, lo:hi] if lo < P else gate_sb[1][:, d, lo - P : hi - P]), ALU.mult)
+            nc.vector.tensor_tensor(pulled[d][:, lo:hi], y_sb[:].indirect(entries(pos_sb[d], lo, hi)), gates[:, d * S + lo : d * S + hi], ALU.mult)
 
         def add(lo, hi):
             nc.vector.tensor_tensor(total[:, lo:hi], pulled[0][:, lo:hi], pulled[1][:, lo:hi], ALU.add)
@@ -139,10 +156,6 @@ def tile_picked_ygcon_relu_p_kernel(
         def finish(lo, hi, queue):
             nc.vector.scalar_tensor_tensor(result[:, lo:hi], total[:, lo:hi], 0.0, base[:, lo:hi], ALU.max, ALU.add)
             queue.dma_start(out=out[:, lo:hi], in_=result[:, lo:hi])
-
-
-        def turn(dst, src, start, stop):
-            nc.tensor.matmul(dst, src, ident[:], start=start, stop=stop, is_transpose=True)
 
         base_turned_ps = psum.tile([P, P], F32, name="base_turned_ps")
         turn(base_turned_ps[:], base[:, 0:P], True, True)

@@ -70,12 +70,12 @@ def tile_picked_ygcon_relu_p_kernel(
         def load_words(g):
             nc.sync.dma_start(out=word_table[g][:], in_=x_words[g].rearrange("p c t -> p (c t)").bitcast(I32))
 
-        load_words(0)
         for q in range(4):
             nc.sync.dma_start(
                 out=scale_table[32 * q : 32 * q + 4 * PASSES, :].bitcast(I32),
                 in_=x_scales[:, 4 * q : 4 * q + 4, :].bitcast(I32),
             )
+        load_words(0)
         for g in range(PASSES):
             nc.sync.dma_start(out=w_raw[g][:], in_=w1[g * P * PACK : (g + 1) * P * PACK, :].rearrange("(p j) m -> p j m", j=PACK))
         load_words(1)
@@ -98,10 +98,10 @@ def tile_picked_ygcon_relu_p_kernel(
                 gates[:].rearrange("p (n t) -> p n t", t=2 * PACK)[:, :, PACK * h : PACK * (h + 1)], spread[:].rearrange("p t n -> p n t"), COPY
             )
 
-        x_first = keep.tile([P, S], U32, name="x_first", align_bytes=64)
-        nc.vector.tensor_copy(x_first[:], word_table[0][:].bitcast(U32).indirect(offs_sb[:]))
         x_scale = keep.tile([P, S], U8, name="x_scale", align_bytes=64)
         nc.vector.tensor_copy(x_scale[:], scale_table[:].indirect(offs_sb[:]))
+        x_first = keep.tile([P, S], U32, name="x_first", align_bytes=64)
+        nc.vector.tensor_copy(x_first[:], word_table[0][:].bitcast(U32).indirect(offs_sb[:]))
 
         w_codes, w_scale = [], []
         for g in range(PASSES):

@@ -59,9 +59,6 @@ def tile_picked_ygcon_relu_p_kernel(
         for q in range(P // QUAD):
             rows = slice(q * QUAD, (q + 1) * QUAD)
             nc.vector.tensor_tensor(ident[rows, rows], col_no[rows, :], row_no[rows, :], ALU.is_equal)
-        nc.sync.dma_start(offs_sb[:], offs)
-        gate_cols = keep.tile([P, 2 * PACK], F32, name="gate_cols")
-        nc.sync.dma_start(out=gate_cols[:], in_=gate.rearrange("d p j -> (d p) j")[P - 1 : P + 1, :].rearrange("r (n t) -> (r n) t", t=2 * PACK))
         nc.scalar.activation(warm_out[:], warm_in[:], COPY)
 
         word_table = [keep.tile([P, T], I32, name="word_table%d" % g, align_bytes=64) for g in range(PASSES)]
@@ -70,14 +67,20 @@ def tile_picked_ygcon_relu_p_kernel(
         def load_words(g):
             nc.sync.dma_start(out=word_table[g][:], in_=x_words[g].rearrange("p c t -> p (c t)").bitcast(I32))
 
+        def load_weights(g):
+            nc.sync.dma_start(out=w_raw[g][:], in_=w1[g * P * PACK : (g + 1) * P * PACK, :].rearrange("(p j) m -> p j m", j=PACK))
+
+        load_weights(0)
+        nc.sync.dma_start(offs_sb[:], offs)
+        gate_cols = keep.tile([P, 2 * PACK], F32, name="gate_cols")
+        nc.sync.dma_start(out=gate_cols[:], in_=gate.rearrange("d p j -> (d p) j")[P - 1 : P + 1, :].rearrange("r (n t) -> (r n) t", t=2 * PACK))
         for q in range(4):
             nc.sync.dma_start(
                 out=scale_table[32 * q : 32 * q + 4 * PASSES, :].bitcast(I32),
                 in_=x_scales[:, 4 * q : 4 * q + 4, :].bitcast(I32),
             )
         load_words(0)
-        for g in range(PASSES):
-            nc.sync.dma_start(out=w_raw[g][:], in_=w1[g * P * PACK : (g + 1) * P * PACK, :].rearrange("(p j) m -> p j m", j=PACK))
+        load_weights(1)
         load_words(1)
         pos0_sb = keep.tile([P, S], F32, name="pos0_sb", tag="sum_slot1")
         vel0_sb = keep.tile([P, S], F32, name="vel0_sb", tag="y_slot")

@@ -98,7 +98,7 @@ def tile_picked_ygcon_relu_p_kernel(
             for t in range(PACK):
                 turn(spread[:, t, :], gate_cols[:, PACK * h + t : PACK * h + t + 1].to_broadcast([P, P]), True, True)
             nc.scalar.activation(
-                gates[:].rearrange("p (n t) -> p n t", t=2 * PACK)[:, :, PACK * h : PACK * (h + 1)], spread[:].rearrange("p t n -> p n t"), COPY
+                gates[:].rearrange("p (n t) -> p n t", t=2 * PACK)[:, :, PACK * h : PACK * (h + 1)], spread[:].rearrange("p t n -> p n t"), COPY, scale=C_FORCE
             )
 
         x_scale = keep.tile([P, S], U8, name="x_scale", align_bytes=64)
@@ -109,7 +109,9 @@ def tile_picked_ygcon_relu_p_kernel(
         w_codes, w_scale = [], []
         for g in range(PASSES):
             grouped = keep.tile([P, N, PACK], BF16, name="w_grouped%d" % g, align_bytes=64)
-            nc.scalar.activation(grouped[:], w_raw[g][:].rearrange("p j m -> p m j"), COPY)
+            nc.scalar.activation(
+                grouped[:].rearrange("p (c i) j -> p c j i", i=PACK), w_raw[g][:].rearrange("p j (c i) -> p c j i", i=PACK), COPY
+            )
             codes = keep.tile([P, N], U32, name="w_codes%d" % g, align_bytes=64)
             plane = keep.tile([P, N], U8, name="w_scale%d" % g, align_bytes=64)
             nc.vector.quantize_mx(out=codes[:].bitcast(FP8X4), scales=plane[:], in_=grouped[:].rearrange("p m j -> p (m j)"))
@@ -141,7 +143,7 @@ def tile_picked_ygcon_relu_p_kernel(
                     stop=last,
                 )
         for i, (lo, hi) in enumerate(Y_PIECES):
-            nc.scalar.activation(y_sb[:, lo:hi], acc[i][:], COPY, scale=C_FORCE)
+            nc.scalar.copy(y_sb[:, lo:hi], acc[i][:])
 
         base = keep.tile([P, S], F32, name="base")
         nc.vector.scalar_tensor_tensor(base[:], pos0_sb[:], C_POS, damped[:], ALU.mult, ALU.add)
@@ -150,11 +152,18 @@ def tile_picked_ygcon_relu_p_kernel(
         total = keep.tile([P, S], F32, name="total")
         result = keep.tile([P, S], F32, name="result")
 
+        mid, cut = S - 64 - P, S - 64
+
+        def neighbours(d, lo, hi):
+            if d == 1 and lo >= cut:
+                return gates[:, S + P : S + P + hi - lo]
+            return pulled[d][:, lo:hi]
+
         def fetch(d, lo, hi):
-            nc.vector.tensor_tensor(pulled[d][:, lo:hi], y_sb[:].indirect(entries(pos_sb[d], lo, hi)), gates[:, d * S + lo : d * S + hi], ALU.mult)
+            nc.vector.tensor_tensor(neighbours(d, lo, hi), y_sb[:].indirect(entries(pos_sb[d], lo, hi)), gates[:, d * S + lo : d * S + hi], ALU.mult)
 
         def add(lo, hi):
-            nc.vector.tensor_tensor(total[:, lo:hi], pulled[0][:, lo:hi], pulled[1][:, lo:hi], ALU.add)
+            nc.vector.tensor_tensor(total[:, lo:hi], neighbours(0, lo, hi), neighbours(1, lo, hi), ALU.add)
 
         def finish(lo, hi, queue):
             nc.vector.scalar_tensor_tensor(result[:, lo:hi], total[:, lo:hi], 0.0, base[:, lo:hi], ALU.max, ALU.add)
@@ -163,7 +172,7 @@ def tile_picked_ygcon_relu_p_kernel(
         base_turned_ps = psum.tile([P, P], F32, name="base_turned_ps")
         turn(base_turned_ps[:], base[:, 0:P], True, True)
         base_turned = keep.tile([P, P], F32, name="base_turned")
-        nc.scalar.activation(base_turned[:], base_turned_ps[:], COPY)
+        nc.scalar.copy(base_turned[:], base_turned_ps[:])
 
         sum_ps = psum.tile([P, P], F32, name="sum_ps")
         out_ps = psum.tile([P, P], F32, name="out_ps")
@@ -176,10 +185,9 @@ def tile_picked_ygcon_relu_p_kernel(
         turn(sum_ps[:], pulled[1][:, 0:P], False, True)
         nc.scalar.activation(force[:], sum_ps[:], RELU)
         turn(out_ps[:], force[:], False, True)
-        nc.scalar.activation(done[:], out_ps[:], COPY)
+        nc.scalar.copy(done[:], out_ps[:])
         nc.sync.dma_start(out=out[:, 0:P], in_=done[:])
 
-        mid, cut = 2 * P, S - 64
         fetch(0, P, S)
         fetch(1, P, mid)
         fetch(1, mid, cut)

@@ -149,52 +149,57 @@ def tile_picked_ygcon_relu_p_kernel(
         nc.vector.scalar_tensor_tensor(base[:], pos0_sb[:], C_POS, damped[:], ALU.mult, ALU.add)
 
         pulled = [keep.tile([P, S], F32, name="pulled%d" % d, tag="sum_slot%d" % d) for d in range(2)]
+        plain = [keep.tile([P, S], F32, name="plain%d" % d) for d in range(2)]
         total = keep.tile([P, S], F32, name="total")
         result = keep.tile([P, S], F32, name="result")
 
         mid, cut = S - 64 - P, S - 64
 
-        def neighbours(d, lo, hi):
-            if d == 1 and lo >= cut:
-                return gates[:, S + P : S + P + hi - lo]
-            return pulled[d][:, lo:hi]
+        def fetch_weighted(d, lo, hi):
+            nc.vector.tensor_tensor(pulled[d][:, lo:hi], y_sb[:].indirect(entries(pos_sb[d], lo, hi)), gates[:, d * S + lo : d * S + hi], ALU.mult)
 
-        def fetch(d, lo, hi):
-            nc.vector.tensor_tensor(neighbours(d, lo, hi), y_sb[:].indirect(entries(pos_sb[d], lo, hi)), gates[:, d * S + lo : d * S + hi], ALU.mult)
+        def fetch_plain(d, lo, hi):
+            nc.scalar.activation(plain[d][:, lo:hi], y_sb[:].indirect(entries(pos_sb[d], lo, hi)), COPY)
+
+        def weigh(d, lo, hi):
+            nc.vector.tensor_tensor(pulled[d][:, lo:hi], plain[d][:, lo:hi], gates[:, d * S + lo : d * S + hi], ALU.mult)
 
         def add(lo, hi):
-            nc.vector.tensor_tensor(total[:, lo:hi], neighbours(0, lo, hi), neighbours(1, lo, hi), ALU.add)
+            nc.vector.tensor_tensor(total[:, lo:hi], pulled[0][:, lo:hi], pulled[1][:, lo:hi], ALU.add)
 
-        def finish(lo, hi, queue):
+        def finish(lo, hi):
             nc.vector.scalar_tensor_tensor(result[:, lo:hi], total[:, lo:hi], 0.0, base[:, lo:hi], ALU.max, ALU.add)
-            queue.dma_start(out=out[:, lo:hi], in_=result[:, lo:hi])
+            nc.sync.dma_start(out=out[:, lo:hi], in_=result[:, lo:hi])
 
         base_turned_ps = psum.tile([P, P], F32, name="base_turned_ps")
-        turn(base_turned_ps[:], base[:, 0:P], True, True)
         base_turned = keep.tile([P, P], F32, name="base_turned")
-        nc.scalar.copy(base_turned[:], base_turned_ps[:])
-
         sum_ps = psum.tile([P, P], F32, name="sum_ps")
         out_ps = psum.tile([P, P], F32, name="out_ps")
         force = keep.tile([P, P], F32, name="force")
         done = keep.tile([P, P], F32, name="done")
-        fetch(0, 0, P)
-        fetch(1, 0, P)
+
+        fetch_plain(0, P, mid)
+        fetch_weighted(0, 0, P)
+        fetch_weighted(1, 0, P)
+        fetch_plain(0, mid, S)
+        turn(base_turned_ps[:], base[:, 0:P], True, True)
+        nc.scalar.copy(base_turned[:], base_turned_ps[:])
         turn(out_ps[:], base_turned[:], True, False)
         turn(sum_ps[:], pulled[0][:, 0:P], True, False)
         turn(sum_ps[:], pulled[1][:, 0:P], False, True)
+        fetch_plain(1, mid, S)
         nc.scalar.activation(force[:], sum_ps[:], RELU)
         turn(out_ps[:], force[:], False, True)
         nc.scalar.copy(done[:], out_ps[:])
         nc.sync.dma_start(out=out[:, 0:P], in_=done[:])
 
-        fetch(0, P, S)
-        fetch(1, P, mid)
-        fetch(1, mid, cut)
+        weigh(0, P, mid)
+        fetch_weighted(1, P, mid)
+        weigh(0, mid, S)
         add(P, mid)
-        fetch(1, cut, S)
+        weigh(1, mid, S)
+        finish(P, mid)
         add(mid, cut)
-        finish(P, mid, nc.sync)
         add(cut, S)
-        finish(mid, cut, nc.sync)
-        finish(cut, S, nc.sync)
+        finish(mid, cut)
+        finish(cut, S)

@@ -155,6 +155,11 @@ def tile_picked_ygcon_relu_p_kernel(
 
         mid, cut = S - 64 - P, S - 64
 
+        def weighted(d, lo, hi):
+            if d == 1 and lo >= mid:
+                return plain[0][:, P + lo - mid : P + hi - mid]
+            return pulled[d][:, lo:hi]
+
         def fetch_weighted(d, lo, hi):
             nc.vector.tensor_tensor(pulled[d][:, lo:hi], y_sb[:].indirect(entries(pos_sb[d], lo, hi)), gates[:, d * S + lo : d * S + hi], ALU.mult)
 
@@ -162,10 +167,10 @@ def tile_picked_ygcon_relu_p_kernel(
             nc.scalar.activation(plain[d][:, lo:hi], y_sb[:].indirect(entries(pos_sb[d], lo, hi)), COPY)
 
         def weigh(d, lo, hi):
-            nc.vector.tensor_tensor(pulled[d][:, lo:hi], plain[d][:, lo:hi], gates[:, d * S + lo : d * S + hi], ALU.mult)
+            nc.vector.tensor_tensor(weighted(d, lo, hi), plain[d][:, lo:hi], gates[:, d * S + lo : d * S + hi], ALU.mult)
 
         def add(lo, hi):
-            nc.vector.tensor_tensor(total[:, lo:hi], pulled[0][:, lo:hi], pulled[1][:, lo:hi], ALU.add)
+            nc.vector.tensor_tensor(total[:, lo:hi], weighted(0, lo, hi), weighted(1, lo, hi), ALU.add)
 
         def finish(lo, hi):
             nc.vector.scalar_tensor_tensor(result[:, lo:hi], total[:, lo:hi], 0.0, base[:, lo:hi], ALU.max, ALU.add)
@@ -184,21 +189,21 @@ def tile_picked_ygcon_relu_p_kernel(
         fetch_plain(0, mid, S)
         turn(base_turned_ps[:], base[:, 0:P], True, True)
         nc.scalar.copy(base_turned[:], base_turned_ps[:])
-        turn(out_ps[:], base_turned[:], True, False)
         turn(sum_ps[:], pulled[0][:, 0:P], True, False)
         turn(sum_ps[:], pulled[1][:, 0:P], False, True)
+        turn(out_ps[:], base_turned[:], True, False)
         fetch_plain(1, mid, S)
         nc.scalar.activation(force[:], sum_ps[:], RELU)
         turn(out_ps[:], force[:], False, True)
         nc.scalar.copy(done[:], out_ps[:])
-        nc.sync.dma_start(out=out[:, 0:P], in_=done[:])
 
-        weigh(0, P, mid)
         fetch_weighted(1, P, mid)
+        weigh(0, P, mid)
         weigh(0, mid, S)
         add(P, mid)
         weigh(1, mid, S)
         finish(P, mid)
+        nc.sync.dma_start(out=out[:, 0:P], in_=done[:])
         add(mid, cut)
         add(cut, S)
         finish(mid, cut)

@@ -85,9 +85,9 @@ def tile_picked_ygcon_relu_p_kernel(
         pos0_sb = keep.tile([P, S], F32, name="pos0_sb", tag="sum_slot1")
         vel0_sb = keep.tile([P, S], F32, name="vel0_sb", tag="y_slot")
         nc.sync.dma_start(out=vel0_sb[:], in_=vel0)
+        nc.sync.dma_start(out=pos0_sb[:], in_=pos0)
         nc.sync.dma_start(pos_sb[0][:], pos1)
         nc.sync.dma_start(pos_sb[1][:], pos2)
-        nc.sync.dma_start(out=pos0_sb[:], in_=pos0)
 
         def turn(dst, src, start, stop):
             nc.tensor.matmul(dst, src, ident[:], start=start, stop=stop, is_transpose=True)
@@ -187,12 +187,12 @@ def tile_picked_ygcon_relu_p_kernel(
         fetch_weighted(0, 0, P)
         fetch_weighted(1, 0, P)
         fetch_plain(0, mid, S)
+        fetch_plain(1, mid, S)
         turn(base_turned_ps[:], base[:, 0:P], True, True)
         nc.scalar.copy(base_turned[:], base_turned_ps[:])
         turn(sum_ps[:], pulled[0][:, 0:P], True, False)
         turn(sum_ps[:], pulled[1][:, 0:P], False, True)
         turn(out_ps[:], base_turned[:], True, False)
-        fetch_plain(1, mid, S)
         nc.scalar.activation(force[:], sum_ps[:], RELU)
         turn(out_ps[:], force[:], False, True)
         nc.scalar.copy(done[:], out_ps[:])

@@ -172,9 +172,9 @@ def tile_picked_ygcon_relu_p_kernel(
         def add(lo, hi):
             nc.vector.tensor_tensor(total[:, lo:hi], weighted(0, lo, hi), weighted(1, lo, hi), ALU.add)
 
-        def finish(lo, hi):
+        def finish(lo, hi, queue):
             nc.vector.scalar_tensor_tensor(result[:, lo:hi], total[:, lo:hi], 0.0, base[:, lo:hi], ALU.max, ALU.add)
-            nc.sync.dma_start(out=out[:, lo:hi], in_=result[:, lo:hi])
+            queue.dma_start(out=out[:, lo:hi], in_=result[:, lo:hi])
 
         base_turned_ps = psum.tile([P, P], F32, name="base_turned_ps")
         base_turned = keep.tile([P, P], F32, name="base_turned")
@@ -202,9 +202,9 @@ def tile_picked_ygcon_relu_p_kernel(
         weigh(0, mid, S)
         add(P, mid)
         weigh(1, mid, S)
-        finish(P, mid)
-        nc.sync.dma_start(out=out[:, 0:P], in_=done[:])
+        finish(P, mid, nc.sync)
+        nc.scalar.dma_start(out=out[:, 0:P], in_=done[:])
         add(mid, cut)
         add(cut, S)
-        finish(mid, cut)
-        finish(cut, S)
+        finish(mid, cut, nc.sync)
+        finish(cut, S, nc.scalar)

@@ -206,5 +206,5 @@ def tile_picked_ygcon_relu_p_kernel(
         nc.scalar.dma_start(out=out[:, 0:P], in_=done[:])
         add(mid, cut)
         add(cut, S)
-        finish(mid, cut, nc.sync)
-        finish(cut, S, nc.scalar)
+        finish(mid, cut, nc.scalar)
+        finish(cut, S, nc.sync)

@@ -153,7 +153,7 @@ def tile_picked_ygcon_relu_p_kernel(
         total = keep.tile([P, S], F32, name="total")
         result = keep.tile([P, S], F32, name="result")
 
-        mid, cut = S - 64 - P, S - 64
+        half, mid, cut = S // 2, S - 64 - P, S - 64
 
         def weighted(d, lo, hi):
             if d == 1 and lo >= mid:
@@ -172,16 +172,14 @@ def tile_picked_ygcon_relu_p_kernel(
         def add(lo, hi):
             nc.vector.tensor_tensor(total[:, lo:hi], weighted(0, lo, hi), weighted(1, lo, hi), ALU.add)
 
-        def finish(lo, hi, queue):
+        def finish(lo, hi):
             nc.vector.scalar_tensor_tensor(result[:, lo:hi], total[:, lo:hi], 0.0, base[:, lo:hi], ALU.max, ALU.add)
-            queue.dma_start(out=out[:, lo:hi], in_=result[:, lo:hi])
 
         base_turned_ps = psum.tile([P, P], F32, name="base_turned_ps")
         base_turned = keep.tile([P, P], F32, name="base_turned")
         sum_ps = psum.tile([P, P], F32, name="sum_ps")
         out_ps = psum.tile([P, P], F32, name="out_ps")
         force = keep.tile([P, P], F32, name="force")
-        done = keep.tile([P, P], F32, name="done")
 
         fetch_plain(0, P, mid)
         fetch_weighted(0, 0, P)
@@ -195,16 +193,18 @@ def tile_picked_ygcon_relu_p_kernel(
         turn(out_ps[:], base_turned[:], True, False)
         nc.scalar.activation(force[:], sum_ps[:], RELU)
         turn(out_ps[:], force[:], False, True)
-        nc.scalar.copy(done[:], out_ps[:])
+        nc.scalar.copy(result[:, 0:P], out_ps[:])
 
         fetch_weighted(1, P, mid)
         weigh(0, P, mid)
         weigh(0, mid, S)
         add(P, mid)
         weigh(1, mid, S)
-        finish(P, mid, nc.sync)
-        nc.scalar.dma_start(out=out[:, 0:P], in_=done[:])
+        finish(P, half)
+        nc.scalar.dma_start(out=out[:, 0:half], in_=result[:, 0:half])
         add(mid, cut)
         add(cut, S)
-        finish(mid, cut, nc.scalar)
-        finish(cut, S, nc.sync)
+        finish(half, mid)
+        finish(mid, cut)
+        finish(cut, S)
+        nc.scalar.dma_start(out=out[:, half:S], in_=result[:, half:S])

@@ -153,11 +153,12 @@ def tile_picked_ygcon_relu_p_kernel(
         total = keep.tile([P, S], F32, name="total")
         result = keep.tile([P, S], F32, name="result")
 
-        half, mid, cut = S // 2, S - 64 - P, S - 64
+        early, mid, cut = 192, S - 192, S - 96
+        block = slice(early, mid)
 
         def weighted(d, lo, hi):
             if d == 1 and lo >= mid:
-                return plain[0][:, P + lo - mid : P + hi - mid]
+                return plain[0][:, lo - mid : hi - mid]
             return pulled[d][:, lo:hi]
 
         def fetch_weighted(d, lo, hi):
@@ -181,30 +182,31 @@ def tile_picked_ygcon_relu_p_kernel(
         out_ps = psum.tile([P, P], F32, name="out_ps")
         force = keep.tile([P, P], F32, name="force")
 
-        fetch_plain(0, P, mid)
-        fetch_weighted(0, 0, P)
-        fetch_weighted(1, 0, P)
+        fetch_plain(0, 0, early)
+        fetch_weighted(0, early, mid)
+        fetch_weighted(1, early, mid)
         fetch_plain(0, mid, S)
         fetch_plain(1, mid, S)
-        turn(base_turned_ps[:], base[:, 0:P], True, True)
+        turn(base_turned_ps[:], base[:, block], True, True)
         nc.scalar.copy(base_turned[:], base_turned_ps[:])
-        turn(sum_ps[:], pulled[0][:, 0:P], True, False)
-        turn(sum_ps[:], pulled[1][:, 0:P], False, True)
+        turn(sum_ps[:], pulled[0][:, block], True, False)
+        turn(sum_ps[:], pulled[1][:, block], False, True)
         turn(out_ps[:], base_turned[:], True, False)
         nc.scalar.activation(force[:], sum_ps[:], RELU)
         turn(out_ps[:], force[:], False, True)
-        nc.scalar.copy(result[:, 0:P], out_ps[:])
+        nc.scalar.copy(result[:, block], out_ps[:])
 
-        fetch_weighted(1, P, mid)
-        weigh(0, P, mid)
+        fetch_weighted(1, 0, early)
+        weigh(0, 0, early)
         weigh(0, mid, S)
-        add(P, mid)
+        add(0, P)
         weigh(1, mid, S)
-        finish(P, half)
-        nc.scalar.dma_start(out=out[:, 0:half], in_=result[:, 0:half])
+        add(P, early)
+        finish(0, P)
         add(mid, cut)
         add(cut, S)
-        finish(half, mid)
+        finish(P, early)
+        nc.sync.dma_start(out=out[:, 0:early], in_=result[:, 0:early])
         finish(mid, cut)
         finish(cut, S)
-        nc.scalar.dma_start(out=out[:, half:S], in_=result[:, half:S])
+        nc.sync.dma_start(out=out[:, early:S], in_=result[:, early:S])

@@ -153,7 +153,7 @@ def tile_picked_ygcon_relu_p_kernel(
         total = keep.tile([P, S], F32, name="total")
         result = keep.tile([P, S], F32, name="result")
 
-        early, mid, cut = 192, S - 192, S - 96
+        step, early, mid, cut = 96, 192, S - 192, S - 96
         block = slice(early, mid)
 
         def weighted(d, lo, hi):
@@ -186,7 +186,8 @@ def tile_picked_ygcon_relu_p_kernel(
         fetch_weighted(0, early, mid)
         fetch_weighted(1, early, mid)
         fetch_plain(0, mid, S)
-        fetch_plain(1, mid, S)
+        fetch_plain(1, mid, cut)
+        fetch_plain(1, cut, S)
         turn(base_turned_ps[:], base[:, block], True, True)
         nc.scalar.copy(base_turned[:], base_turned_ps[:])
         turn(sum_ps[:], pulled[0][:, block], True, False)
@@ -197,15 +198,17 @@ def tile_picked_ygcon_relu_p_kernel(
         nc.scalar.copy(result[:, block], out_ps[:])
 
         fetch_weighted(1, 0, early)
-        weigh(0, 0, early)
+        weigh(0, 0, step)
+        weigh(0, step, early)
         weigh(0, mid, S)
-        add(0, P)
-        weigh(1, mid, S)
-        add(P, early)
-        finish(0, P)
+        add(0, step)
+        weigh(1, mid, cut)
+        add(step, early)
+        weigh(1, cut, S)
+        finish(0, step)
         add(mid, cut)
         add(cut, S)
-        finish(P, early)
+        finish(step, early)
         nc.sync.dma_start(out=out[:, 0:early], in_=result[:, 0:early])
         finish(mid, cut)
         finish(cut, S)

@@ -82,7 +82,7 @@ def tile_picked_ygcon_relu_p_kernel(
         load_words(0)
         load_weights(1)
         load_words(1)
-        pos0_sb = keep.tile([P, S], F32, name="pos0_sb", tag="sum_slot1")
+        pos0_sb = keep.tile([P, S], F32, name="pos0_sb")
         vel0_sb = keep.tile([P, S], F32, name="vel0_sb", tag="y_slot")
         nc.sync.dma_start(out=vel0_sb[:], in_=vel0)
         nc.sync.dma_start(out=pos0_sb[:], in_=pos0)
@@ -118,7 +118,7 @@ def tile_picked_ygcon_relu_p_kernel(
             w_codes.append(codes)
             w_scale.append(plane)
 
-        damped = keep.tile([P, S], F32, name="damped", tag="sum_slot0")
+        damped = keep.tile([P, S], F32, name="damped")
         nc.scalar.activation(damped[:], vel0_sb[:], COPY, scale=C_VEL)
 
         y_sb = keep.tile([P, S], F32, name="y_sb", tag="y_slot")
@@ -148,12 +148,12 @@ def tile_picked_ygcon_relu_p_kernel(
         base = keep.tile([P, S], F32, name="base")
         nc.vector.scalar_tensor_tensor(base[:], pos0_sb[:], C_POS, damped[:], ALU.mult, ALU.add)
 
-        pulled = [keep.tile([P, S], F32, name="pulled%d" % d, tag="sum_slot%d" % d) for d in range(2)]
+        pulled = [keep.tile([P, S], F32, name="pulled%d" % d) for d in range(2)]
         plain = [keep.tile([P, S], F32, name="plain%d" % d) for d in range(2)]
         total = keep.tile([P, S], F32, name="total")
         result = keep.tile([P, S], F32, name="result")
 
-        step, early, mid, cut = 96, 192, S - 192, S - 96
+        step, early, mid, cut, last = 112, 224, S - 160, S - 80, S - 64
         block = slice(early, mid)
 
         def weighted(d, lo, hi):
@@ -186,8 +186,8 @@ def tile_picked_ygcon_relu_p_kernel(
         fetch_weighted(0, early, mid)
         fetch_weighted(1, early, mid)
         fetch_plain(0, mid, S)
-        fetch_plain(1, mid, cut)
-        fetch_plain(1, cut, S)
+        fetch_plain(1, mid, last)
+        fetch_plain(1, last, S)
         turn(base_turned_ps[:], base[:, block], True, True)
         nc.scalar.copy(base_turned[:], base_turned_ps[:])
         turn(sum_ps[:], pulled[0][:, block], True, False)
@@ -202,9 +202,9 @@ def tile_picked_ygcon_relu_p_kernel(
         weigh(0, step, early)
         weigh(0, mid, S)
         add(0, step)
-        weigh(1, mid, cut)
+        weigh(1, mid, last)
+        weigh(1, last, S)
         add(step, early)
-        weigh(1, cut, S)
         finish(0, step)
         add(mid, cut)
         add(cut, S)

@@ -153,13 +153,8 @@ def tile_picked_ygcon_relu_p_kernel(
         total = keep.tile([P, S], F32, name="total")
         result = keep.tile([P, S], F32, name="result")
 
-        step, early, mid, cut, last = 112, 224, S - 160, S - 80, S - 64
-        block = slice(early, mid)
-
-        def weighted(d, lo, hi):
-            if d == 1 and lo >= mid:
-                return plain[0][:, lo - mid : hi - mid]
-            return pulled[d][:, lo:hi]
+        step, early, fused, mid = 112, 224, 256, S - P
+        block = slice(mid, S)
 
         def fetch_weighted(d, lo, hi):
             nc.vector.tensor_tensor(pulled[d][:, lo:hi], y_sb[:].indirect(entries(pos_sb[d], lo, hi)), gates[:, d * S + lo : d * S + hi], ALU.mult)
@@ -168,10 +163,10 @@ def tile_picked_ygcon_relu_p_kernel(
             nc.scalar.activation(plain[d][:, lo:hi], y_sb[:].indirect(entries(pos_sb[d], lo, hi)), COPY)
 
         def weigh(d, lo, hi):
-            nc.vector.tensor_tensor(weighted(d, lo, hi), plain[d][:, lo:hi], gates[:, d * S + lo : d * S + hi], ALU.mult)
+            nc.vector.tensor_tensor(pulled[d][:, lo:hi], plain[d][:, lo:hi], gates[:, d * S + lo : d * S + hi], ALU.mult)
 
         def add(lo, hi):
-            nc.vector.tensor_tensor(total[:, lo:hi], weighted(0, lo, hi), weighted(1, lo, hi), ALU.add)
+            nc.vector.tensor_tensor(total[:, lo:hi], pulled[0][:, lo:hi], pulled[1][:, lo:hi], ALU.add)
 
         def finish(lo, hi):
             nc.vector.scalar_tensor_tensor(result[:, lo:hi], total[:, lo:hi], 0.0, base[:, lo:hi], ALU.max, ALU.add)
@@ -182,12 +177,10 @@ def tile_picked_ygcon_relu_p_kernel(
         out_ps = psum.tile([P, P], F32, name="out_ps")
         force = keep.tile([P, P], F32, name="force")
 
-        fetch_plain(0, 0, early)
-        fetch_weighted(0, early, mid)
-        fetch_weighted(1, early, mid)
-        fetch_plain(0, mid, S)
-        fetch_plain(1, mid, last)
-        fetch_plain(1, last, S)
+        fetch_plain(0, 0, mid)
+        fetch_weighted(0, mid, S)
+        fetch_weighted(1, mid, S)
+        fetch_plain(1, fused, mid)
         turn(base_turned_ps[:], base[:, block], True, True)
         nc.scalar.copy(base_turned[:], base_turned_ps[:])
         turn(sum_ps[:], pulled[0][:, block], True, False)
@@ -197,19 +190,15 @@ def tile_picked_ygcon_relu_p_kernel(
         turn(out_ps[:], force[:], False, True)
         nc.scalar.copy(result[:, block], out_ps[:])
 
-        fetch_weighted(1, 0, early)
-        weigh(0, 0, step)
-        weigh(0, step, early)
-        weigh(0, mid, S)
+        fetch_weighted(1, 0, fused)
+        weigh(0, 0, early)
+        weigh(0, early, mid)
+        weigh(1, fused, mid)
         add(0, step)
-        weigh(1, mid, last)
-        weigh(1, last, S)
         add(step, early)
+        add(early, mid)
         finish(0, step)
-        add(mid, cut)
-        add(cut, S)
         finish(step, early)
         nc.sync.dma_start(out=out[:, 0:early], in_=result[:, 0:early])
-        finish(mid, cut)
-        finish(cut, S)
+        finish(early, mid)
         nc.sync.dma_start(out=out[:, early:S], in_=result[:, early:S])

@@ -153,7 +153,7 @@ def tile_picked_ygcon_relu_p_kernel(
         total = keep.tile([P, S], F32, name="total")
         result = keep.tile([P, S], F32, name="result")
 
-        step, early, fused, mid = 112, 224, 256, S - P
+        step, early, fused, mid = 128, 256, 256, S - P
         block = slice(mid, S)
 
         def fetch_weighted(d, lo, hi):

@@ -109,9 +109,12 @@ def tile_picked_ygcon_relu_p_kernel(
         w_codes, w_scale = [], []
         for g in range(PASSES):
             grouped = keep.tile([P, N, PACK], BF16, name="w_grouped%d" % g, align_bytes=64)
-            nc.scalar.activation(
-                grouped[:].rearrange("p (c i) j -> p c j i", i=PACK), w_raw[g][:].rearrange("p j (c i) -> p c j i", i=PACK), COPY
-            )
+            rounded = grouped[:].rearrange("p (c i) j -> p c j i", i=PACK)
+            loaded = w_raw[g][:].rearrange("p j (c i) -> p c j i", i=PACK)
+            if g == 0:
+                nc.vector.tensor_copy(rounded, loaded)
+            else:
+                nc.scalar.activation(rounded, loaded, COPY)
             codes = keep.tile([P, N], U32, name="w_codes%d" % g, align_bytes=64)
             plane = keep.tile([P, N], U8, name="w_scale%d" % g, align_bytes=64)
             nc.vector.quantize_mx(out=codes[:].bitcast(FP8X4), scales=plane[:], in_=grouped[:].rearrange("p m j -> p (m j)"))

@@ -83,7 +83,7 @@ def tile_picked_ygcon_relu_p_kernel(
         load_weights(1)
         load_words(1)
         pos0_sb = keep.tile([P, S], F32, name="pos0_sb")
-        vel0_sb = keep.tile([P, S], F32, name="vel0_sb", tag="y_slot")
+        vel0_sb = keep.tile([P, S], F32, name="vel0_sb")
         nc.sync.dma_start(out=vel0_sb[:], in_=vel0)
         nc.sync.dma_start(out=pos0_sb[:], in_=pos0)
         nc.sync.dma_start(pos_sb[0][:], pos1)
@@ -122,9 +122,10 @@ def tile_picked_ygcon_relu_p_kernel(
             w_scale.append(plane)
 
         damped = keep.tile([P, S], F32, name="damped")
-        nc.scalar.activation(damped[:], vel0_sb[:], COPY, scale=C_VEL)
+        half = S // 2
+        nc.scalar.activation(damped[:, 0:half], vel0_sb[:, 0:half], COPY, scale=C_VEL)
 
-        y_sb = keep.tile([P, S], F32, name="y_sb", tag="y_slot")
+        y_sb = keep.tile([P, S], F32, name="y_sb")
         acc = [psum.tile([P, hi - lo], F32, name="acc%d" % lo) for lo, hi in Y_PIECES]
         x_late = keep.tile([P, S], U32, name="x_late", tag="w_slot1", align_bytes=64)
         x_codes = [
@@ -149,7 +150,9 @@ def tile_picked_ygcon_relu_p_kernel(
             nc.scalar.copy(y_sb[:, lo:hi], acc[i][:])
 
         base = keep.tile([P, S], F32, name="base")
-        nc.vector.scalar_tensor_tensor(base[:], pos0_sb[:], C_POS, damped[:], ALU.mult, ALU.add)
+        nc.vector.tensor_scalar(damped[:, half:S], vel0_sb[:, half:S], C_VEL, None, ALU.mult)
+        for lo in (0, half):
+            nc.vector.scalar_tensor_tensor(base[:, lo : lo + half], pos0_sb[:, lo : lo + half], C_POS, damped[:, lo : lo + half], ALU.mult, ALU.add)
 
         pulled = [keep.tile([P, S], F32, name="pulled%d" % d) for d in range(2)]
         plain = [keep.tile([P, S], F32, name="plain%d" % d) for d in range(2)]
@@ -175,7 +178,7 @@ def tile_picked_ygcon_relu_p_kernel(
             nc.vector.scalar_tensor_tensor(result[:, lo:hi], total[:, lo:hi], 0.0, base[:, lo:hi], ALU.max, ALU.add)
 
         base_turned_ps = psum.tile([P, P], F32, name="base_turned_ps")
-        base_turned = keep.tile([P, P], F32, name="base_turned")
+        base_turned = gates[:, S + mid : 2 * S]
         sum_ps = psum.tile([P, P], F32, name="sum_ps")
         out_ps = psum.tile([P, P], F32, name="out_ps")
         force = keep.tile([P, P], F32, name="force")
@@ -185,10 +188,10 @@ def tile_picked_ygcon_relu_p_kernel(
         fetch_weighted(1, mid, S)
         fetch_plain(1, fused, mid)
         turn(base_turned_ps[:], base[:, block], True, True)
-        nc.scalar.copy(base_turned[:], base_turned_ps[:])
+        nc.scalar.copy(base_turned, base_turned_ps[:])
         turn(sum_ps[:], pulled[0][:, block], True, False)
         turn(sum_ps[:], pulled[1][:, block], False, True)
-        turn(out_ps[:], base_turned[:], True, False)
+        turn(out_ps[:], base_turned, True, False)
         nc.scalar.activation(force[:], sum_ps[:], RELU)
         turn(out_ps[:], force[:], False, True)
         nc.scalar.copy(result[:, block], out_ps[:])

from contextlib import ExitStack

import concourse.mybir as mybir

K, T, S, N = 1024, 1024, 512, 128
FLOPS = 2 * K * N * S

F32 = mybir.dt.float32
BF16 = mybir.dt.bfloat16
I32 = mybir.dt.int32
U32 = mybir.dt.uint32
U16 = mybir.dt.uint16
U8 = mybir.dt.uint8
FP8X4 = mybir.dt.float8_e4m3fn_x4
ALU = mybir.AluOpType
COPY = mybir.ActivationFunctionType.Copy
RELU = mybir.ActivationFunctionType.Relu

P = 128
PACK = 4
QUAD = 32
PASSES = K // (P * PACK)
LIST_COL = 16
DT = 0.7
C_FORCE = DT * DT
C_POS = 1.0 - DT * DT
C_VEL = DT - 0.5 * DT * DT
Y_PIECES = ((0, 256), (256, 384), (384, 512))


def entries(list_tile, lo, hi):
    return list_tile[:, lo // LIST_COL : hi // LIST_COL]


def tile_picked_ygcon_relu_p_kernel(
    tc, x_words, x_scales, w1, gate, pos0, vel0, offs, pos1, pos2, out
):
    nc = tc.nc
    with ExitStack() as ctx:
        keep = ctx.enter_context(tc.tile_pool(name="keep", bufs=1))
        psum = ctx.enter_context(tc.psum_pool(name="psum", bufs=1))

        offs_sb = keep.tile([P, S // LIST_COL], U16, name="offs_sb")
        pos_sb = [keep.tile([P, S // LIST_COL], U16, name="pos_sb%d" % d) for d in range(2)]
        scale_table = keep.tile([P, T], U8, name="scale_table", align_bytes=64)
        warm_in = keep.tile([P, 1], F32, name="warm_in")
        warm_out = keep.tile([P, 1], F32, name="warm_out")

        nc.vector.memset(scale_table[:].bitcast(I32), 0)
        nc.vector.memset(warm_in[:], 0.0)
        ident = keep.tile([P, P], F32, name="ident")
        nc.vector.memset(ident[:], 0.0)
        ones = keep.tile([P, QUAD], F32, name="ones")
        col_no = keep.tile([P, QUAD], F32, name="col_no", align_bytes=64)
        row_no = keep.tile([P, QUAD], F32, name="row_no", align_bytes=64)
        nc.vector.memset(ones[:], 1.0)
        nc.vector.tensor_tensor_scan(col_no[:], ones[:], ones[:], 0.0, ALU.mult, ALU.add)
        nc.vector.transpose(row_no[:], col_no[:])
        for q in range(P // QUAD):
            rows = slice(q * QUAD, (q + 1) * QUAD)
            nc.vector.tensor_tensor(ident[rows, rows], col_no[rows, :], row_no[rows, :], ALU.is_equal)
        nc.scalar.activation(warm_out[:], warm_in[:], COPY)

        word_table = [keep.tile([P, T], I32, name="word_table%d" % g, align_bytes=64) for g in range(PASSES)]
        w_raw = [keep.tile([P, PACK, N], F32, name="w_raw%d" % g, tag="w_slot%d" % g, align_bytes=64) for g in range(PASSES)]

        def load_words(g):
            nc.sync.dma_start(out=word_table[g][:], in_=x_words[g].rearrange("p c t -> p (c t)").bitcast(I32))

        def load_weights(g):
            nc.sync.dma_start(out=w_raw[g][:], in_=w1[g * P * PACK : (g + 1) * P * PACK, :].rearrange("(p j) m -> p j m", j=PACK))

        load_weights(0)
        nc.sync.dma_start(offs_sb[:], offs)
        gate_cols = keep.tile([P, 2 * PACK], F32, name="gate_cols")
        nc.sync.dma_start(out=gate_cols[:], in_=gate.rearrange("d p j -> (d p) j")[P - 1 : P + 1, :].rearrange("r (n t) -> (r n) t", t=2 * PACK))
        for q in range(4):
            nc.sync.dma_start(
                out=scale_table[32 * q : 32 * q + 4 * PASSES, :].bitcast(I32),
                in_=x_scales[:, 4 * q : 4 * q + 4, :].bitcast(I32),
            )
        load_words(0)
        load_weights(1)
        load_words(1)
        pos0_sb = keep.tile([P, S], F32, name="pos0_sb")
        vel0_sb = keep.tile([P, S], F32, name="vel0_sb")
        nc.sync.dma_start(out=vel0_sb[:], in_=vel0)
        nc.sync.dma_start(out=pos0_sb[:], in_=pos0)
        nc.sync.dma_start(pos_sb[0][:], pos1)
        nc.sync.dma_start(pos_sb[1][:], pos2)

        def turn(dst, src, start, stop):
            nc.tensor.matmul(dst, src, ident[:], start=start, stop=stop, is_transpose=True)

        gates = keep.tile([P, 2 * S], F32, name="gates")
        for h in range(2):
            spread = psum.tile([P, PACK, P], F32, name="spread%d" % h)
            for t in range(PACK):
                turn(spread[:, t, :], gate_cols[:, PACK * h + t : PACK * h + t + 1].to_broadcast([P, P]), True, True)
            nc.scalar.activation(
                gates[:].rearrange("p (n t) -> p n t", t=2 * PACK)[:, :, PACK * h : PACK * (h + 1)], spread[:].rearrange("p t n -> p n t"), COPY, scale=C_FORCE
            )

        x_scale = keep.tile([P, S], U8, name="x_scale", align_bytes=64)
        nc.vector.tensor_copy(x_scale[:], scale_table[:].indirect(offs_sb[:]))
        x_first = keep.tile([P, S], U32, name="x_first", align_bytes=64)
        nc.vector.tensor_copy(x_first[:], word_table[0][:].bitcast(U32).indirect(offs_sb[:]))

        w_codes, w_scale = [], []
        for g in range(PASSES):
            grouped = keep.tile([P, N, PACK], BF16, name="w_grouped%d" % g, align_bytes=64)
            rounded = grouped[:].rearrange("p (c i) j -> p c j i", i=PACK)
            loaded = w_raw[g][:].rearrange("p j (c i) -> p c j i", i=PACK)
            if g == 0:
                nc.vector.tensor_copy(rounded, loaded)
            else:
                nc.scalar.activation(rounded, loaded, COPY)
            codes = keep.tile([P, N], U32, name="w_codes%d" % g, align_bytes=64)
            plane = keep.tile([P, N], U8, name="w_scale%d" % g, align_bytes=64)
            nc.vector.quantize_mx(out=codes[:].bitcast(FP8X4), scales=plane[:], in_=grouped[:].rearrange("p m j -> p (m j)"))
            w_codes.append(codes)
            w_scale.append(plane)

        damped = keep.tile([P, S], F32, name="damped")
        half = S // 2
        nc.scalar.activation(damped[:, 0:half], vel0_sb[:, 0:half], COPY, scale=C_VEL)

        y_sb = keep.tile([P, S], F32, name="y_sb")
        acc = [psum.tile([P, hi - lo], F32, name="acc%d" % lo) for lo, hi in Y_PIECES]
        x_late = keep.tile([P, S], U32, name="x_late", tag="w_slot1", align_bytes=64)
        x_codes = [
            [x_first[:, lo:hi] for lo, hi in Y_PIECES],
            [x_late[:, lo:hi] for lo, hi in Y_PIECES],
        ]
        for g in range(PASSES):
            last = g == PASSES - 1
            for i, (lo, hi) in enumerate(Y_PIECES if last else ()):
                nc.vector.tensor_copy(x_codes[g][i], word_table[g][:].bitcast(U32).indirect(entries(offs_sb, lo, hi)))
            for i, (lo, hi) in enumerate(Y_PIECES):
                nc.tensor.matmul_mx(
                    out=acc[i][:],
                    lhsT=w_codes[g][:].bitcast(FP8X4),
                    lhsT_scale=w_scale[g][:],
                    rhs=x_codes[g][i].bitcast(FP8X4),
                    rhs_scale=x_scale[4 * g : P, lo:hi],
                    start=(g == 0),
                    stop=last,
                )
        for i, (lo, hi) in enumerate(Y_PIECES):
            nc.scalar.copy(y_sb[:, lo:hi], acc[i][:])

        base = keep.tile([P, S], F32, name="base")
        nc.vector.tensor_scalar(damped[:, half:S], vel0_sb[:, half:S], C_VEL, None, ALU.mult)
        for lo in (0, half):
            nc.vector.scalar_tensor_tensor(base[:, lo : lo + half], pos0_sb[:, lo : lo + half], C_POS, damped[:, lo : lo + half], ALU.mult, ALU.add)

        pulled = [keep.tile([P, S], F32, name="pulled%d" % d) for d in range(2)]
        plain = [keep.tile([P, S], F32, name="plain%d" % d) for d in range(2)]
        total = keep.tile([P, S], F32, name="total")
        result = keep.tile([P, S], F32, name="result")

        step, early, fused, mid = 128, 256, 256, S - P
        block = slice(mid, S)

        def fetch_weighted(d, lo, hi):
            nc.vector.tensor_tensor(pulled[d][:, lo:hi], y_sb[:].indirect(entries(pos_sb[d], lo, hi)), gates[:, d * S + lo : d * S + hi], ALU.mult)

        def fetch_plain(d, lo, hi):
            nc.scalar.activation(plain[d][:, lo:hi], y_sb[:].indirect(entries(pos_sb[d], lo, hi)), COPY)

        def weigh(d, lo, hi):
            nc.vector.tensor_tensor(pulled[d][:, lo:hi], plain[d][:, lo:hi], gates[:, d * S + lo : d * S + hi], ALU.mult)

        def add(lo, hi):
            nc.vector.tensor_tensor(total[:, lo:hi], pulled[0][:, lo:hi], pulled[1][:, lo:hi], ALU.add)

        def finish(lo, hi):
            nc.vector.scalar_tensor_tensor(result[:, lo:hi], total[:, lo:hi], 0.0, base[:, lo:hi], ALU.max, ALU.add)

        base_turned_ps = psum.tile([P, P], F32, name="base_turned_ps")
        base_turned = gates[:, S + mid : 2 * S]
        sum_ps = psum.tile([P, P], F32, name="sum_ps")
        out_ps = psum.tile([P, P], F32, name="out_ps")
        force = keep.tile([P, P], F32, name="force")

        fetch_plain(0, 0, mid)
        fetch_weighted(0, mid, S)
        fetch_weighted(1, mid, S)
        fetch_plain(1, fused, mid)
        turn(base_turned_ps[:], base[:, block], True, True)
        nc.scalar.copy(base_turned, base_turned_ps[:])
        turn(sum_ps[:], pulled[0][:, block], True, False)
        turn(sum_ps[:], pulled[1][:, block], False, True)
        turn(out_ps[:], base_turned, True, False)
        nc.scalar.activation(force[:], sum_ps[:], RELU)
        turn(out_ps[:], force[:], False, True)
        nc.scalar.copy(result[:, block], out_ps[:])

        fetch_weighted(1, 0, fused)
        weigh(0, 0, early)
        weigh(0, early, mid)
        weigh(1, fused, mid)
        add(0, step)
        add(step, early)
        add(early, mid)
        finish(0, step)
        finish(step, early)
        nc.sync.dma_start(out=out[:, 0:early], in_=result[:, 0:early])
        finish(early, mid)
        nc.sync.dma_start(out=out[:, early:S], in_=result[:, early:S])
